import numpy as np
import ml_dtypes


def mxq(x, axis, fmt="e4m3"):
    dtype, down = {"e4m3": (ml_dtypes.float8_e4m3fn, 7), "e5m2": (ml_dtypes.float8_e5m2, 14)}[fmt]
    v = np.moveaxis(np.asarray(x, np.float32).astype(ml_dtypes.bfloat16).astype(np.float64), axis, -1)
    blocks = v.reshape(v.shape[:-1] + (-1, 32))
    amax = np.abs(blocks).max(-1, keepdims=True)
    byte = np.maximum(np.where(amax > 0, np.frexp(amax)[1] - 1 + 127, 0) - down, 1)
    scale = np.exp2(byte - 127.0)
    codes = (blocks / scale).astype(np.float32).astype(dtype).astype(np.float64)
    return np.moveaxis((codes * scale).reshape(v.shape), -1, axis)


WIDE = False


def mx_kscale(k):
    if not WIDE:
        return np.ones(k)
    levels = np.array([10, -10, 5, -5, 0])
    if k % 512:
        return np.exp2(np.random.permutation(np.resize(levels, k // 32))).repeat(32)
    a = np.empty((k // 512, 16))
    for p in range(k // 512):
        a[p, :8] = np.random.permutation(np.resize(levels, 8))
        for g in range(8):
            far = levels[np.abs(levels - a[p, g]) >= 10]
            a[p, g + 8] = far[np.random.randint(len(far))]
    return np.exp2(a.ravel()).repeat(32)


def f64(x):
    return np.asarray(x).astype(np.float64)


def striped8(idx):
    return np.concatenate([v.reshape(-1, 16).T for v in idx]).astype(np.uint16)


def unstriped8(offs):
    return np.stack([offs[16 * g:16 * g + 16].T.reshape(-1) for g in range(8)]).astype(np.int64)


E2M1 = np.array([0.0, 0.5, 1.0, 1.5, 2.0, 3.0, 4.0, 6.0, -0.0, -0.5, -1.0, -1.5, -2.0, -3.0, -4.0, -6.0])


def pack_weight(w, fmt):
    k, n = w.shape
    w = f64(np.asarray(w, np.float32).astype(ml_dtypes.bfloat16)).reshape(k // 32, 32, n)
    amax = np.abs(w).max(1)
    if fmt == "e4m3":
        byte = np.frexp(amax)[1] - 1 + 127 - 7
    else:
        mant, ex = np.frexp(amax / 6.0)
        byte = np.where(mant > 0.5, ex, ex - 1) + 127
    byte = np.clip(np.where(amax > 0, byte, 1), 1, 254)
    scaled = (w * np.exp2(127.0 - byte)[:, None, :]).reshape(k, n).astype(np.float32)
    by_word = np.ascontiguousarray(scaled.reshape(k // 512, 128, 4, n).transpose(0, 1, 3, 2))
    if fmt == "e4m3":
        words = by_word.astype(ml_dtypes.float8_e4m3fn).view(np.uint8)
    else:
        c = by_word.astype(ml_dtypes.float4_e2m1fn).view(np.uint8) & 0xF
        words = (c[..., 0::2] | (c[..., 1::2] << 4)).reshape(k // 512, 128, 2 * n)
    return np.ascontiguousarray(words), np.ascontiguousarray(byte.astype(np.uint8).reshape(k // 512, 16, n))


def unpack_weight(words, scales, fmt):
    g, _, n = scales.shape
    words = np.ascontiguousarray(words).reshape(g, 128, n, -1)
    if fmt == "e4m3":
        vals = words.view(ml_dtypes.float8_e4m3fn).astype(np.float64)
    else:
        nib = np.empty((g, 128, n, 4), np.uint8)
        nib[..., 0::2] = words & 0xF
        nib[..., 1::2] = words >> 4
        vals = E2M1[nib]
    vals = vals * np.repeat(np.exp2(scales.astype(np.float64) - 127.0), 8, axis=1)[..., None]
    return vals.transpose(0, 1, 3, 2).reshape(g * 512, n)


K, M, T, S = 1536, 256, 1024, 512


def setup_inputs():
    n = np.random.standard_normal
    s = mx_kscale(K)[:, None]
    p_w = pack_weight(n((K, M)) / np.sqrt(K) / s, "e2m1")
    return {
        "xT": (n((K, T)) * s).astype(np.float32),
        "w_words": p_w[0],
        "w_scales": p_w[1],
        "wgt": np.repeat(np.random.uniform(0.5, 2.0, (8, S)), 16, axis=0).astype(np.float32),
        "wgo": np.repeat(np.random.uniform(0.5, 2.0, (8, S)), 16, axis=0).astype(np.float32),
        "offs": striped8(np.stack([np.random.permutation(T)[:S] for _ in range(8)])),
        "offs2": striped8(np.stack([np.random.permutation(T)[:S] for _ in range(8)])),
    }


def reference(xT, w_words, w_scales, wgt, wgo, offs, offs2):
    idx = unstriped8(offs)
    group = np.arange(K) % 512 // 64
    xg = f64(wgt)[np.arange(K) // 4 % 128] * f64(xT)[np.arange(K)[:, None], idx[group]]
    xT_ = mxq(xg, 0, "e4m3")
    w_ = unpack_weight(w_words, w_scales, "e2m1")
    y = w_.T @ xT_
    place = unstriped8(offs2)[np.arange(M) % 128 // 16]
    out = np.zeros((M, T))
    out[np.arange(M)[:, None], place] = f64(wgo)[np.arange(M) % 128] * (y)
    return out

@@ -1,0 +1,173 @@
+from contextlib import ExitStack
+
+import concourse.mybir as mybir
+
+K, M, T, S = 1536, 256, 1024, 512
+P = 128
+PACK = 4
+PASSES = K // (P * PACK)
+HALVES = 2
+SH = S // HALVES
+NQ = 128
+M_TILES = M // P
+
+FLOPS = 2 * K * M * S
+
+F32 = mybir.dt.float32
+BF16 = mybir.dt.bfloat16
+I32 = mybir.dt.int32
+U32 = mybir.dt.uint32
+U16 = mybir.dt.uint16
+U8 = mybir.dt.uint8
+E4M3 = mybir.dt.float8_e4m3fn_x4
+E2M1 = mybir.dt.float4_e2m1fn_x4
+MULT = mybir.AluOpType.mult
+
+
+def tile_list_hboth_none_kernel(tc, xT, w_words, w_scales, wgt, wgo, offs, offs2, out):
+    nc = tc.nc
+    with ExitStack() as ctx:
+        lists = ctx.enter_context(tc.tile_pool(name="lists", bufs=1))
+        keep = ctx.enter_context(tc.tile_pool(name="keep", bufs=1))
+        psum = ctx.enter_context(tc.psum_pool(name="psum", bufs=1))
+
+        gather_list = lists.tile([P, S // 16], U16, name="gather_list")
+        scatter_list = lists.tile([P, S // 16], U16, name="scatter_list")
+        wgt_sb = [keep.tile([P, SH], F32, name=f"wgt{h}") for h in range(HALVES)]
+        wgo_sb = [keep.tile([P, SH], F32, name=f"wgo{h}") for h in range(HALVES)]
+        words = keep.tile([P, PASSES, 2 * M], U8, name="words", align_bytes=64)
+        wsc = keep.tile([P, PASSES, M], U8, name="wsc", align_bytes=64)
+        plane = [[keep.tile([P, T], F32, name=f"plane{a}_{i}") for i in range(PACK)] for a in range(PASSES)]
+        picked = [[keep.tile([P, PACK, SH], F32, name=f"picked{a}_{h}") for h in range(HALVES)] for a in range(PASSES)]
+        grouped = [
+            [keep.tile([P, SH, PACK], BF16, name=f"grouped{a}_{h}", align_bytes=64) for h in range(HALVES)]
+            for a in range(PASSES)
+        ]
+        codes = [[keep.tile([P, SH], U32, name=f"codes{a}_{h}", align_bytes=64) for h in range(HALVES)] for a in range(PASSES)]
+        xsc = [[keep.tile([P, SH], U8, name=f"xsc{a}_{h}", align_bytes=64) for h in range(HALVES)] for a in range(PASSES)]
+        y = [[keep.tile([P, SH], F32, name=f"y{m}_{h}") for h in range(HALVES)] for m in range(M_TILES)]
+        window = [keep.tile([P, T], F32, name=f"window{m}") for m in range(M_TILES)]
+        acc = [
+            [[psum.tile([P, NQ], F32, name=f"acc{m}_{h}_{q}") for q in range(SH // NQ)] for h in range(HALVES)]
+            for m in range(M_TILES)
+        ]
+
+        def load_plane(a, i):
+            rows = xT[a * P * PACK : (a + 1) * P * PACK, :].rearrange("(p j) t -> p j t", j=PACK)
+            nc.sync.dma_start(plane[a][i][:], rows[:, i, :])
+
+        def gather(a, i, h):
+            nc.vector.tensor_tensor(
+                picked[a][h][:, i, :],
+                plane[a][i][:].indirect(gather_list[:, h * SH // 16 : (h + 1) * SH // 16]),
+                wgt_sb[h][:],
+                MULT,
+            )
+
+        def group(a, h):
+            nc.scalar.copy(grouped[a][h][:], picked[a][h][:].rearrange("p j s -> p s j"))
+
+        def quantise(a, h):
+            nc.vector.quantize_mx(
+                out=codes[a][h][:].bitcast(E4M3),
+                scales=xsc[a][h][:],
+                in_=grouped[a][h][:].rearrange("p s j -> p (s j)"),
+            )
+
+        def multiply(a, h):
+            for m in range(M_TILES):
+                for q in range(SH // NQ):
+                    nc.tensor.matmul_mx(
+                        out=acc[m][h][q][:],
+                        lhsT=words[:, a, 2 * P * m : 2 * P * (m + 1)].bitcast(E2M1),
+                        lhsT_scale=wsc[:, a, P * m : P * (m + 1)],
+                        rhs=codes[a][h][:, NQ * q : NQ * (q + 1)].bitcast(E4M3),
+                        rhs_scale=xsc[a][h][:, NQ * q : NQ * (q + 1)],
+                        start=(a == 0),
+                        stop=(a == PASSES - 1),
+                    )
+
+        def empty(m, h):
+            for q in range(SH // NQ):
+                nc.scalar.copy(y[m][h][:, NQ * q : NQ * (q + 1)], acc[m][h][q][:])
+
+        def scatter(m, h):
+            nc.vector.tensor_tensor(
+                window[m][:].indirect(scatter_list[:, h * SH // 16 : (h + 1) * SH // 16]),
+                y[m][h][:],
+                wgo_sb[h][:],
+                MULT,
+            )
+
+        nc.sync.dma_start(gather_list[:], offs)
+        nc.scalar.dma_start(wgt_sb[0][:], wgt[:, 0:SH])
+        load_plane(0, 0)
+        nc.sync.dma_start(wgt_sb[1][:], wgt[:, SH:S])
+        nc.vector.memset(wsc[:].rearrange("p a n -> p (a n)").bitcast(I32), 0)
+        for m in range(M_TILES):
+            nc.vector.memset(window[m][:], 0.0)
+        for i in range(1, PACK):
+            load_plane(0, i)
+        for i in range(PACK):
+            load_plane(1, i)
+        nc.sync.dma_start(
+            words[:].rearrange("p a b -> p (a b)").bitcast(I32).rearrange("p (a b) -> p a b", a=PASSES),
+            w_words.rearrange("a p b -> p a b").bitcast(I32),
+        )
+        for i in range(PACK):
+            load_plane(2, i)
+        nc.sync.dma_start(scatter_list[:], offs2)
+        for h in range(HALVES):
+            nc.sync.dma_start(wgo_sb[h][:], wgo[:, h * SH : (h + 1) * SH])
+        for quad in range(4):
+            nc.scalar.dma_start(
+                wsc[32 * quad : 32 * quad + 4, :, :].bitcast(I32),
+                w_scales[:, 4 * quad : 4 * quad + 4, :].rearrange("a r n -> r a n").bitcast(I32),
+            )
+
+        for i in range(PACK):
+            for h in range(HALVES):
+                gather(0, i, h)
+        for h in range(HALVES):
+            group(0, h)
+        for i in range(2):
+            for h in range(HALVES):
+                gather(1, i, h)
+        quantise(0, 0)
+        quantise(0, 1)
+        for h in range(HALVES):
+            multiply(0, h)
+        gather(1, 2, 0)
+        gather(1, 2, 1)
+        gather(1, 3, 0)
+        group(1, 0)
+        gather(2, 0, 0)
+        gather(2, 1, 0)
+        quantise(1, 0)
+        multiply(1, 0)
+        gather(2, 2, 0)
+        gather(2, 3, 0)
+        group(2, 0)
+        gather(1, 3, 1)
+        group(1, 1)
+        gather(2, 0, 1)
+        gather(2, 1, 1)
+        quantise(2, 0)
+        multiply(2, 0)
+        empty(0, 0)
+        empty(1, 0)
+        gather(2, 2, 1)
+        quantise(1, 1)
+        multiply(1, 1)
+        gather(2, 3, 1)
+        group(2, 1)
+        scatter(0, 0)
+        quantise(2, 1)
+        multiply(2, 1)
+        empty(0, 1)
+        empty(1, 1)
+        scatter(1, 0)
+        scatter(0, 1)
+        nc.sync.dma_start(out[0:P, :], window[0][:])
+        scatter(1, 1)
+        nc.sync.dma_start(out[P:M, :], window[1][:])

@@ -39,12 +39,9 @@ def tile_list_hboth_none_kernel(tc, xT, w_words, w_scales, wgt, wgo, offs, offs2
         wsc = keep.tile([P, PASSES, M], U8, name="wsc", align_bytes=64)
         plane = [[keep.tile([P, T], F32, name=f"plane{a}_{i}") for i in range(PACK)] for a in range(PASSES)]
         picked = [[keep.tile([P, PACK, SH], F32, name=f"picked{a}_{h}") for h in range(HALVES)] for a in range(PASSES)]
-        grouped = [
-            [keep.tile([P, SH, PACK], BF16, name=f"grouped{a}_{h}", align_bytes=64) for h in range(HALVES)]
-            for a in range(PASSES)
-        ]
-        codes = [[keep.tile([P, SH], U32, name=f"codes{a}_{h}", align_bytes=64) for h in range(HALVES)] for a in range(PASSES)]
-        xsc = [[keep.tile([P, SH], U8, name=f"xsc{a}_{h}", align_bytes=64) for h in range(HALVES)] for a in range(PASSES)]
+        grouped = [keep.tile([P, S, PACK], BF16, name=f"grouped{a}", align_bytes=64) for a in range(PASSES)]
+        codes = [keep.tile([P, S], U32, name=f"codes{a}", align_bytes=64) for a in range(PASSES)]
+        xsc = [keep.tile([P, S], U8, name=f"xsc{a}", align_bytes=64) for a in range(PASSES)]
         y = [[keep.tile([P, SH], F32, name=f"y{m}_{h}") for h in range(HALVES)] for m in range(M_TILES)]
         window = [keep.tile([P, T], F32, name=f"window{m}") for m in range(M_TILES)]
         acc = [
@@ -65,13 +62,16 @@ def tile_list_hboth_none_kernel(tc, xT, w_words, w_scales, wgt, wgo, offs, offs2
             )
 
         def group(a, h):
-            nc.scalar.copy(grouped[a][h][:], picked[a][h][:].rearrange("p j s -> p s j"))
+            nc.scalar.copy(
+                grouped[a][:, h * SH : (h + 1) * SH, :].rearrange("p (c i) j -> p c j i", i=4),
+                picked[a][h][:].rearrange("p j (c i) -> p c j i", i=4),
+            )
 
-        def quantise(a, h):
+        def quantise(a, first, last):
             nc.vector.quantize_mx(
-                out=codes[a][h][:].bitcast(E4M3),
-                scales=xsc[a][h][:],
-                in_=grouped[a][h][:].rearrange("p s j -> p (s j)"),
+                out=codes[a][:, first:last].bitcast(E4M3),
+                scales=xsc[a][:, first:last],
+                in_=grouped[a][:, first:last, :].rearrange("p s j -> p (s j)"),
             )
 
         def multiply(a, h):
@@ -81,8 +81,8 @@ def tile_list_hboth_none_kernel(tc, xT, w_words, w_scales, wgt, wgo, offs, offs2
                         out=acc[m][h][q][:],
                         lhsT=words[:, a, 2 * P * m : 2 * P * (m + 1)].bitcast(E2M1),
                         lhsT_scale=wsc[:, a, P * m : P * (m + 1)],
-                        rhs=codes[a][h][:, NQ * q : NQ * (q + 1)].bitcast(E4M3),
-                        rhs_scale=xsc[a][h][:, NQ * q : NQ * (q + 1)],
+                        rhs=codes[a][:, h * SH + NQ * q : h * SH + NQ * (q + 1)].bitcast(E4M3),
+                        rhs_scale=xsc[a][:, h * SH + NQ * q : h * SH + NQ * (q + 1)],
                         start=(a == 0),
                         stop=(a == PASSES - 1),
                     )
@@ -99,31 +99,27 @@ def tile_list_hboth_none_kernel(tc, xT, w_words, w_scales, wgt, wgo, offs, offs2
                 MULT,
             )
 
-        nc.sync.dma_start(gather_list[:], offs)
-        nc.scalar.dma_start(wgt_sb[0][:], wgt[:, 0:SH])
-        load_plane(0, 0)
-        nc.sync.dma_start(wgt_sb[1][:], wgt[:, SH:S])
         nc.vector.memset(wsc[:].rearrange("p a n -> p (a n)").bitcast(I32), 0)
         for m in range(M_TILES):
             nc.vector.memset(window[m][:], 0.0)
-        for i in range(1, PACK):
-            load_plane(0, i)
-        for i in range(PACK):
-            load_plane(1, i)
-        nc.sync.dma_start(
-            words[:].rearrange("p a b -> p (a b)").bitcast(I32).rearrange("p (a b) -> p a b", a=PASSES),
-            w_words.rearrange("a p b -> p a b").bitcast(I32),
-        )
-        for i in range(PACK):
-            load_plane(2, i)
-        nc.sync.dma_start(scatter_list[:], offs2)
-        for h in range(HALVES):
-            nc.sync.dma_start(wgo_sb[h][:], wgo[:, h * SH : (h + 1) * SH])
+        nc.sync.dma_start(gather_list[:], offs)
+        nc.sync.dma_start(wgt_sb[0][:], wgt[:, 0:SH])
+        load_plane(0, 0)
+        nc.sync.dma_start(wgt_sb[1][:], wgt[:, SH:S])
         for quad in range(4):
             nc.scalar.dma_start(
                 wsc[32 * quad : 32 * quad + 4, :, :].bitcast(I32),
                 w_scales[:, 4 * quad : 4 * quad + 4, :].rearrange("a r n -> r a n").bitcast(I32),
             )
+        for c in range(1, PASSES * PACK):
+            load_plane(c // PACK, c % PACK)
+        nc.sync.dma_start(
+            words[:].rearrange("p a b -> p (a b)").bitcast(I32).rearrange("p (a b) -> p a b", a=PASSES),
+            w_words.rearrange("a p b -> p a b").bitcast(I32),
+        )
+        nc.sync.dma_start(scatter_list[:], offs2)
+        for h in range(HALVES):
+            nc.sync.dma_start(wgo_sb[h][:], wgo[:, h * SH : (h + 1) * SH])
 
         for i in range(PACK):
             for h in range(HALVES):
@@ -133,41 +129,37 @@ def tile_list_hboth_none_kernel(tc, xT, w_words, w_scales, wgt, wgo, offs, offs2
         for i in range(2):
             for h in range(HALVES):
                 gather(1, i, h)
-        quantise(0, 0)
-        quantise(0, 1)
+        quantise(0, 0, S)
         for h in range(HALVES):
             multiply(0, h)
-        gather(1, 2, 0)
-        gather(1, 2, 1)
-        gather(1, 3, 0)
-        group(1, 0)
+        for i in range(2, PACK):
+            for h in range(HALVES):
+                gather(1, i, h)
+        for h in range(HALVES):
+            group(1, h)
         gather(2, 0, 0)
         gather(2, 1, 0)
-        quantise(1, 0)
-        multiply(1, 0)
         gather(2, 2, 0)
+        quantise(1, 0, S)
+        for h in range(HALVES):
+            multiply(1, h)
         gather(2, 3, 0)
         group(2, 0)
-        gather(1, 3, 1)
-        group(1, 1)
         gather(2, 0, 1)
         gather(2, 1, 1)
-        quantise(2, 0)
+        quantise(2, 0, SH)
         multiply(2, 0)
-        empty(0, 0)
-        empty(1, 0)
+        for m in range(M_TILES):
+            empty(m, 0)
         gather(2, 2, 1)
-        quantise(1, 1)
-        multiply(1, 1)
         gather(2, 3, 1)
         group(2, 1)
         scatter(0, 0)
-        quantise(2, 1)
+        quantise(2, SH, S)
         multiply(2, 1)
-        empty(0, 1)
-        empty(1, 1)
+        for m in range(M_TILES):
+            empty(m, 1)
         scatter(1, 0)
-        scatter(0, 1)
-        nc.sync.dma_start(out[0:P, :], window[0][:])
-        scatter(1, 1)
-        nc.sync.dma_start(out[P:M, :], window[1][:])
+        for m in range(M_TILES):
+            scatter(m, 1)
+            nc.sync.dma_start(out[P * m : P * (m + 1), :], window[m][:])

@@ -61,10 +61,10 @@ def tile_list_hboth_none_kernel(tc, xT, w_words, w_scales, wgt, wgo, offs, offs2
                 MULT,
             )
 
-        def group(a, h):
+        def group(a, h, first, count):
             nc.scalar.copy(
-                grouped[a][:, h * SH : (h + 1) * SH, :].rearrange("p (c i) j -> p c j i", i=4),
-                picked[a][h][:].rearrange("p j (c i) -> p c j i", i=4),
+                grouped[a][:, h * SH : (h + 1) * SH, first : first + count].rearrange("p (c i) j -> p c j i", i=4),
+                picked[a][h][:, first : first + count, :].rearrange("p j (c i) -> p c j i", i=4),
             )
 
         def quantise(a, first, last):
@@ -99,9 +99,9 @@ def tile_list_hboth_none_kernel(tc, xT, w_words, w_scales, wgt, wgo, offs, offs2
                 MULT,
             )
 
-        nc.vector.memset(wsc[:].rearrange("p a n -> p (a n)").bitcast(I32), 0)
+        nc.gpsimd.memset(wsc[:].rearrange("p a n -> p (a n)").bitcast(I32), 0)
         for m in range(M_TILES):
-            nc.vector.memset(window[m][:], 0.0)
+            nc.gpsimd.memset(window[m][:], 0.0)
         nc.sync.dma_start(gather_list[:], offs)
         nc.sync.dma_start(wgt_sb[0][:], wgt[:, 0:SH])
         load_plane(0, 0)
@@ -125,7 +125,7 @@ def tile_list_hboth_none_kernel(tc, xT, w_words, w_scales, wgt, wgo, offs, offs2
             for h in range(HALVES):
                 gather(0, i, h)
         for h in range(HALVES):
-            group(0, h)
+            group(0, h, 0, PACK)
         for i in range(2):
             for h in range(HALVES):
                 gather(1, i, h)
@@ -136,24 +136,26 @@ def tile_list_hboth_none_kernel(tc, xT, w_words, w_scales, wgt, wgo, offs, offs2
             for h in range(HALVES):
                 gather(1, i, h)
         for h in range(HALVES):
-            group(1, h)
+            group(1, h, 0, PACK)
         gather(2, 0, 0)
         gather(2, 1, 0)
+        group(2, 0, 0, 2)
         gather(2, 2, 0)
         quantise(1, 0, S)
         for h in range(HALVES):
             multiply(1, h)
         gather(2, 3, 0)
-        group(2, 0)
+        group(2, 0, 2, 2)
         gather(2, 0, 1)
         gather(2, 1, 1)
+        group(2, 1, 0, 2)
         quantise(2, 0, SH)
         multiply(2, 0)
         for m in range(M_TILES):
             empty(m, 0)
         gather(2, 2, 1)
         gather(2, 3, 1)
-        group(2, 1)
+        group(2, 1, 2, 2)
         scatter(0, 0)
         quantise(2, SH, S)
         multiply(2, 1)

from contextlib import ExitStack

import concourse.mybir as mybir

K, M, T, S = 1536, 256, 1024, 512
P = 128
PACK = 4
PASSES = K // (P * PACK)
HALVES = 2
SH = S // HALVES
NQ = 128
M_TILES = M // P

FLOPS = 2 * K * M * S

F32 = mybir.dt.float32
BF16 = mybir.dt.bfloat16
I32 = mybir.dt.int32
U32 = mybir.dt.uint32
U16 = mybir.dt.uint16
U8 = mybir.dt.uint8
E4M3 = mybir.dt.float8_e4m3fn_x4
E2M1 = mybir.dt.float4_e2m1fn_x4
MULT = mybir.AluOpType.mult


def tile_list_hboth_none_kernel(tc, xT, w_words, w_scales, wgt, wgo, offs, offs2, out):
    nc = tc.nc
    with ExitStack() as ctx:
        lists = ctx.enter_context(tc.tile_pool(name="lists", bufs=1))
        keep = ctx.enter_context(tc.tile_pool(name="keep", bufs=1))
        psum = ctx.enter_context(tc.psum_pool(name="psum", bufs=1))

        gather_list = lists.tile([P, S // 16], U16, name="gather_list")
        scatter_list = lists.tile([P, S // 16], U16, name="scatter_list")
        wgt_sb = [keep.tile([P, SH], F32, name=f"wgt{h}") for h in range(HALVES)]
        wgo_sb = [keep.tile([P, SH], F32, name=f"wgo{h}") for h in range(HALVES)]
        words = keep.tile([P, PASSES, 2 * M], U8, name="words", align_bytes=64)
        wsc = keep.tile([P, PASSES, M], U8, name="wsc", align_bytes=64)
        plane = [[keep.tile([P, T], F32, name=f"plane{a}_{i}") for i in range(PACK)] for a in range(PASSES)]
        picked = [[keep.tile([P, PACK, SH], F32, name=f"picked{a}_{h}") for h in range(HALVES)] for a in range(PASSES)]
        grouped = [keep.tile([P, S, PACK], BF16, name=f"grouped{a}", align_bytes=64) for a in range(PASSES)]
        codes = [keep.tile([P, S], U32, name=f"codes{a}", align_bytes=64) for a in range(PASSES)]
        xsc = [keep.tile([P, S], U8, name=f"xsc{a}", align_bytes=64) for a in range(PASSES)]
        y = [[keep.tile([P, SH], F32, name=f"y{m}_{h}") for h in range(HALVES)] for m in range(M_TILES)]
        window = [keep.tile([P, T], F32, name=f"window{m}") for m in range(M_TILES)]
        acc = [
            [[psum.tile([P, NQ], F32, name=f"acc{m}_{h}_{q}") for q in range(SH // NQ)] for h in range(HALVES)]
            for m in range(M_TILES)
        ]

        def load_plane(a, i):
            rows = xT[a * P * PACK : (a + 1) * P * PACK, :].rearrange("(p j) t -> p j t", j=PACK)
            nc.sync.dma_start(plane[a][i][:], rows[:, i, :])

        def gather(a, i, h):
            nc.vector.tensor_tensor(
                picked[a][h][:, i, :],
                plane[a][i][:].indirect(gather_list[:, h * SH // 16 : (h + 1) * SH // 16]),
                wgt_sb[h][:],
                MULT,
            )

        def group(a, h, first, count):
            nc.scalar.copy(
                grouped[a][:, h * SH : (h + 1) * SH, first : first + count].rearrange("p (c i) j -> p c j i", i=4),
                picked[a][h][:, first : first + count, :].rearrange("p j (c i) -> p c j i", i=4),
            )

        def quantise(a, first, last):
            nc.vector.quantize_mx(
                out=codes[a][:, first:last].bitcast(E4M3),
                scales=xsc[a][:, first:last],
                in_=grouped[a][:, first:last, :].rearrange("p s j -> p (s j)"),
            )

        def multiply(a, h):
            for m in range(M_TILES):
                for q in range(SH // NQ):
                    nc.tensor.matmul_mx(
                        out=acc[m][h][q][:],
                        lhsT=words[:, a, 2 * P * m : 2 * P * (m + 1)].bitcast(E2M1),
                        lhsT_scale=wsc[:, a, P * m : P * (m + 1)],
                        rhs=codes[a][:, h * SH + NQ * q : h * SH + NQ * (q + 1)].bitcast(E4M3),
                        rhs_scale=xsc[a][:, h * SH + NQ * q : h * SH + NQ * (q + 1)],
                        start=(a == 0),
                        stop=(a == PASSES - 1),
                    )

        def empty(m, h):
            for q in range(SH // NQ):
                nc.scalar.copy(y[m][h][:, NQ * q : NQ * (q + 1)], acc[m][h][q][:])

        def scatter(m, h):
            nc.vector.tensor_tensor(
                window[m][:].indirect(scatter_list[:, h * SH // 16 : (h + 1) * SH // 16]),
                y[m][h][:],
                wgo_sb[h][:],
                MULT,
            )

        nc.gpsimd.memset(wsc[:].rearrange("p a n -> p (a n)").bitcast(I32), 0)
        for m in range(M_TILES):
            nc.gpsimd.memset(window[m][:], 0.0)
        nc.sync.dma_start(gather_list[:], offs)
        nc.sync.dma_start(wgt_sb[0][:], wgt[:, 0:SH])
        load_plane(0, 0)
        nc.sync.dma_start(wgt_sb[1][:], wgt[:, SH:S])
        for quad in range(4):
            nc.scalar.dma_start(
                wsc[32 * quad : 32 * quad + 4, :, :].bitcast(I32),
                w_scales[:, 4 * quad : 4 * quad + 4, :].rearrange("a r n -> r a n").bitcast(I32),
            )
        for c in range(1, PASSES * PACK):
            load_plane(c // PACK, c % PACK)
        nc.sync.dma_start(
            words[:].rearrange("p a b -> p (a b)").bitcast(I32).rearrange("p (a b) -> p a b", a=PASSES),
            w_words.rearrange("a p b -> p a b").bitcast(I32),
        )
        nc.sync.dma_start(scatter_list[:], offs2)
        for h in range(HALVES):
            nc.sync.dma_start(wgo_sb[h][:], wgo[:, h * SH : (h + 1) * SH])

        for i in range(PACK):
            for h in range(HALVES):
                gather(0, i, h)
        for h in range(HALVES):
            group(0, h, 0, PACK)
        for i in range(2):
            for h in range(HALVES):
                gather(1, i, h)
        quantise(0, 0, S)
        for h in range(HALVES):
            multiply(0, h)
        for i in range(2, PACK):
            for h in range(HALVES):
                gather(1, i, h)
        for h in range(HALVES):
            group(1, h, 0, PACK)
        gather(2, 0, 0)
        gather(2, 1, 0)
        group(2, 0, 0, 2)
        gather(2, 2, 0)
        quantise(1, 0, S)
        for h in range(HALVES):
            multiply(1, h)
        gather(2, 3, 0)
        group(2, 0, 2, 2)
        gather(2, 0, 1)
        gather(2, 1, 1)
        group(2, 1, 0, 2)
        quantise(2, 0, SH)
        multiply(2, 0)
        for m in range(M_TILES):
            empty(m, 0)
        gather(2, 2, 1)
        gather(2, 3, 1)
        group(2, 1, 2, 2)
        scatter(0, 0)
        quantise(2, SH, S)
        multiply(2, 1)
        for m in range(M_TILES):
            empty(m, 1)
        scatter(1, 0)
        for m in range(M_TILES):
            scatter(m, 1)
            nc.sync.dma_start(out[P * m : P * (m + 1), :], window[m][:])
